import numpy as np
import ml_dtypes


def mxq(x, axis, fmt="e4m3"):
    dtype, down = {"e4m3": (ml_dtypes.float8_e4m3fn, 7), "e5m2": (ml_dtypes.float8_e5m2, 14)}[fmt]
    v = np.moveaxis(np.asarray(x, np.float32).astype(ml_dtypes.bfloat16).astype(np.float64), axis, -1)
    blocks = v.reshape(v.shape[:-1] + (-1, 32))
    amax = np.abs(blocks).max(-1, keepdims=True)
    byte = np.maximum(np.where(amax > 0, np.frexp(amax)[1] - 1 + 127, 0) - down, 1)
    scale = np.exp2(byte - 127.0)
    codes = (blocks / scale).astype(np.float32).astype(dtype).astype(np.float64)
    return np.moveaxis((codes * scale).reshape(v.shape), -1, axis)


WIDE = False


def mx_kscale(k):
    if not WIDE:
        return np.ones(k)
    levels = np.array([10, -10, 5, -5, 0])
    if k % 512:
        return np.exp2(np.random.permutation(np.resize(levels, k // 32))).repeat(32)
    a = np.empty((k // 512, 16))
    for p in range(k // 512):
        a[p, :8] = np.random.permutation(np.resize(levels, 8))
        for g in range(8):
            far = levels[np.abs(levels - a[p, g]) >= 10]
            a[p, g + 8] = far[np.random.randint(len(far))]
    return np.exp2(a.ravel()).repeat(32)


def f64(x):
    return np.asarray(x).astype(np.float64)


def striped(idx):
    return np.tile(idx.reshape(-1, 16).T, (8, 1)).astype(np.uint16)


def unstriped(offs):
    return offs[:16].T.reshape(-1).astype(np.int64)


E2M1 = np.array([0.0, 0.5, 1.0, 1.5, 2.0, 3.0, 4.0, 6.0, -0.0, -0.5, -1.0, -1.5, -2.0, -3.0, -4.0, -6.0])


def pack_weight(w, fmt):
    k, n = w.shape
    w = f64(np.asarray(w, np.float32).astype(ml_dtypes.bfloat16)).reshape(k // 32, 32, n)
    amax = np.abs(w).max(1)
    if fmt == "e4m3":
        byte = np.frexp(amax)[1] - 1 + 127 - 7
    else:
        mant, ex = np.frexp(amax / 6.0)
        byte = np.where(mant > 0.5, ex, ex - 1) + 127
    byte = np.clip(np.where(amax > 0, byte, 1), 1, 254)
    scaled = (w * np.exp2(127.0 - byte)[:, None, :]).reshape(k, n).astype(np.float32)
    by_word = np.ascontiguousarray(scaled.reshape(k // 512, 128, 4, n).transpose(0, 1, 3, 2))
    if fmt == "e4m3":
        words = by_word.astype(ml_dtypes.float8_e4m3fn).view(np.uint8)
    else:
        c = by_word.astype(ml_dtypes.float4_e2m1fn).view(np.uint8) & 0xF
        words = (c[..., 0::2] | (c[..., 1::2] << 4)).reshape(k // 512, 128, 2 * n)
    return np.ascontiguousarray(words), np.ascontiguousarray(byte.astype(np.uint8).reshape(k // 512, 16, n))


def unpack_weight(words, scales, fmt):
    g, _, n = scales.shape
    words = np.ascontiguousarray(words).reshape(g, 128, n, -1)
    if fmt == "e4m3":
        vals = words.view(ml_dtypes.float8_e4m3fn).astype(np.float64)
    else:
        nib = np.empty((g, 128, n, 4), np.uint8)
        nib[..., 0::2] = words & 0xF
        nib[..., 1::2] = words >> 4
        vals = E2M1[nib]
    vals = vals * np.repeat(np.exp2(scales.astype(np.float64) - 127.0), 8, axis=1)[..., None]
    return vals.transpose(0, 1, 3, 2).reshape(g * 512, n)


def pack_table(v):
    words, scales = pack_weight(v, "e4m3")
    return np.concatenate([words.reshape(words.shape[0], -1), scales.reshape(scales.shape[0], -1)], axis=1)


def unpack_table(tab):
    g, t = tab.shape[0], tab.shape[1] // 528
    return unpack_weight(tab[:, :512 * t].reshape(g, 128, t, 4), tab[:, 512 * t:].reshape(g, 16, t), "e4m3")


K, M, T, S = 2048, 256, 512, 256


def setup_inputs():
    n = np.random.standard_normal
    s = mx_kscale(K)[:, None]
    return {
        "tab": pack_table(n((K, T)) * s),
        "w": (n((K, M)) / np.sqrt(K) / s).astype(np.float32),
        "b": (0.3 * n(256)).astype(np.float32),
        "offs": striped(np.random.permutation(T)[:S]),
    }


def reference(tab, w, b, offs):
    tab_ = unpack_table(tab)[:, unstriped(offs)]
    w_ = mxq(f64(w), 0, "e4m3")
    y = tab_.T @ w_
    return y + f64(b)[None, :]

from contextlib import ExitStack

import concourse.mybir as mybir
from concourse.masks import make_identity

K, N, T, S = 2048, 256, 512, 256

P = 128
PACK = 4
K_PASS = P * PACK
PASSES = K // K_PASS
WORD_BYTES = K_PASS * T
J_TILES = S // P

F32 = mybir.dt.float32
BF16 = mybir.dt.bfloat16
I32 = mybir.dt.int32
U32 = mybir.dt.uint32
U16 = mybir.dt.uint16
U8 = mybir.dt.uint8
FP8X4 = mybir.dt.float8_e4m3fn_x4

FLOPS = 2 * K * N * S
BYTES = 4 * K * N + (K + K // 32) * S + 4 * N + 2 * P * (S // 16) + 4 * S * N

SPLIT = 160


def tile_list_tabw_tm_bias_kernel(tc, tab, w, b, offs, out):
    nc = tc.nc
    add = mybir.AluOpType.add
    with ExitStack() as ctx:
        keep = ctx.enter_context(tc.tile_pool(name="keep", bufs=1))
        psum = ctx.enter_context(tc.psum_pool(name="psum", bufs=1))

        offsets = keep.tile([P, S // 16], U16)
        table_scales = keep.tile([P, T // 4], I32, align_bytes=64)
        bias_column = keep.tile([P, N // P], F32)
        identity = keep.tile([P, P], F32)
        bias = keep.tile([P, N], F32)
        words = [keep.tile([P, T], U32, name=f"words{a}", align_bytes=64) for a in range(PASSES)]
        w_raw = [keep.tile([P, PACK, N], F32, name=f"w_raw{a}", align_bytes=64) for a in range(PASSES)]
        w_bf16 = [keep.tile([P, N, PACK], BF16, name=f"w_bf16_{a}", align_bytes=64) for a in range(PASSES)]
        w_codes = [keep.tile([P, N], U32, name=f"w_codes{a}", align_bytes=64) for a in range(PASSES)]
        w_scales = [keep.tile([P, N], U8, name=f"w_scales{a}", align_bytes=64) for a in range(PASSES)]
        picked = [keep.tile([P, S], U32, name=f"picked{a}", align_bytes=64) for a in range(PASSES)]
        picked_scales = keep.tile([P, S], U8, align_bytes=64)
        result = [keep.tile([P, N], F32, name=f"result{j}") for j in range(J_TILES)]
        acc = [psum.tile([P, N], F32, name=f"acc{j}") for j in range(J_TILES)]
        bias_bank = psum.tile([P, N // P, P], F32)

        def load_words(a):
            rows = tab[a, 0:WORD_BYTES].bitcast(I32).rearrange("(p t) -> p t", p=P)
            nc.sync.dma_start(out=words[a][:].bitcast(I32), in_=rows)

        def load_w(a):
            rows = w[a * K_PASS : (a + 1) * K_PASS, :]
            nc.sync.dma_start(out=w_raw[a][:], in_=rows.rearrange("(p i) n -> p i n", i=PACK))

        def interleave(copy, a, cols):
            copy(out=w_bf16[a][:, cols, :], in_=w_raw[a][:, :, cols].rearrange("p i n -> p n i"))

        def quantise(a):
            nc.vector.quantize_mx(
                out=w_codes[a][:].bitcast(FP8X4),
                scales=w_scales[a][:],
                in_=w_bf16[a][:].rearrange("p n i -> p (n i)"),
            )

        def gather(a, j0, j1):
            nc.vector.tensor_copy(picked[a][:, j0:j1], words[a][:].indirect(offsets[:, j0 // 16 : j1 // 16]))

        def multiply(a, j):
            cols = slice(j * P, (j + 1) * P)
            nc.tensor.matmul_mx(
                out=acc[j][:],
                lhsT=picked[a][:, cols].bitcast(FP8X4),
                lhsT_scale=picked_scales[4 * a : P, cols],
                rhs=w_codes[a][:].bitcast(FP8X4),
                rhs_scale=w_scales[a][:],
                start=(a == 0),
                stop=(a == PASSES - 1),
            )

        nc.vector.memset(table_scales[:], 0)
        nc.sync.dma_start(offsets[:], offs)
        load_words(0)
        scale_rows = tab[:, WORD_BYTES : WORD_BYTES + 16 * T].bitcast(I32).rearrange("a (q t) -> a q t", q=16)
        for quad in range(4):
            nc.scalar.dma_start(
                out=table_scales[32 * quad : 32 * quad + 16, :],
                in_=scale_rows[:, 4 * quad : 4 * quad + 4, :],
            )
        load_w(0)
        load_w(1)
        nc.scalar.dma_start(out=bias_column[:], in_=b.rearrange("(p h) -> p h", h=N // P))
        load_words(1)
        load_w(2)
        load_w(3)
        load_words(2)
        load_words(3)

        make_identity(nc, identity[:])
        for h in range(N // P):
            nc.tensor.transpose(bias_bank[:, h, :], bias_column[:, h : h + 1].to_broadcast([P, P]), identity[:])
        nc.scalar.copy(out=bias[:].rearrange("p (q h) -> p q h", h=N // P), in_=bias_bank[:].rearrange("p h q -> p q h"))

        nc.vector.tensor_copy(picked_scales[:], table_scales[:].bitcast(U8).indirect(offsets[:]))
        gather(0, 0, S)

        def prepare(a):
            interleave(nc.scalar.copy, a, slice(0, SPLIT))
            interleave(nc.vector.tensor_copy, a, slice(SPLIT, N))

        prepare(0)
        prepare(1)
        quantise(0)
        for j in range(J_TILES):
            multiply(0, j)
        gather(1, 0, S)
        quantise(1)
        prepare(2)
        for j in range(J_TILES):
            multiply(1, j)
        prepare(3)
        quantise(2)
        gather(2, 0, S)
        quantise(3)
        for j in range(J_TILES):
            multiply(2, j)
        for j in range(J_TILES):
            gather(3, j * P, (j + 1) * P)
            multiply(3, j)
        for j in range(J_TILES):
            nc.vector.tensor_tensor(result[j][:], acc[j][:], bias[:], add)
            store = nc.sync if j == 0 else nc.scalar
            store.dma_start(out=out[j * P : (j + 1) * P, :], in_=result[j][:])
